import numpy as np
import ml_dtypes


def mxq(x, axis, fmt="e4m3"):
    dtype, down = {"e4m3": (ml_dtypes.float8_e4m3fn, 7), "e5m2": (ml_dtypes.float8_e5m2, 14)}[fmt]
    v = np.moveaxis(np.asarray(x, np.float32).astype(ml_dtypes.bfloat16).astype(np.float64), axis, -1)
    blocks = v.reshape(v.shape[:-1] + (-1, 32))
    amax = np.abs(blocks).max(-1, keepdims=True)
    byte = np.maximum(np.where(amax > 0, np.frexp(amax)[1] - 1 + 127, 0) - down, 1)
    scale = np.exp2(byte - 127.0)
    codes = (blocks / scale).astype(np.float32).astype(dtype).astype(np.float64)
    return np.moveaxis((codes * scale).reshape(v.shape), -1, axis)


WIDE = False


def mx_kscale(k):
    if not WIDE:
        return np.ones(k)
    levels = np.array([10, -10, 5, -5, 0])
    if k % 512:
        return np.exp2(np.random.permutation(np.resize(levels, k // 32))).repeat(32)
    a = np.empty((k // 512, 16))
    for p in range(k // 512):
        a[p, :8] = np.random.permutation(np.resize(levels, 8))
        for g in range(8):
            far = levels[np.abs(levels - a[p, g]) >= 10]
            a[p, g + 8] = far[np.random.randint(len(far))]
    return np.exp2(a.ravel()).repeat(32)


def f64(x):
    return np.asarray(x).astype(np.float64)


def striped(idx):
    return np.tile(idx.reshape(-1, 16).T, (8, 1)).astype(np.uint16)


def unstriped(offs):
    return offs[:16].T.reshape(-1).astype(np.int64)


E2M1 = np.array([0.0, 0.5, 1.0, 1.5, 2.0, 3.0, 4.0, 6.0, -0.0, -0.5, -1.0, -1.5, -2.0, -3.0, -4.0, -6.0])


def pack_weight(w, fmt):
    k, n = w.shape
    w = f64(np.asarray(w, np.float32).astype(ml_dtypes.bfloat16)).reshape(k // 32, 32, n)
    amax = np.abs(w).max(1)
    if fmt == "e4m3":
        byte = np.frexp(amax)[1] - 1 + 127 - 7
    else:
        mant, ex = np.frexp(amax / 6.0)
        byte = np.where(mant > 0.5, ex, ex - 1) + 127
    byte = np.clip(np.where(amax > 0, byte, 1), 1, 254)
    scaled = (w * np.exp2(127.0 - byte)[:, None, :]).reshape(k, n).astype(np.float32)
    by_word = np.ascontiguousarray(scaled.reshape(k // 512, 128, 4, n).transpose(0, 1, 3, 2))
    if fmt == "e4m3":
        words = by_word.astype(ml_dtypes.float8_e4m3fn).view(np.uint8)
    else:
        c = by_word.astype(ml_dtypes.float4_e2m1fn).view(np.uint8) & 0xF
        words = (c[..., 0::2] | (c[..., 1::2] << 4)).reshape(k // 512, 128, 2 * n)
    return np.ascontiguousarray(words), np.ascontiguousarray(byte.astype(np.uint8).reshape(k // 512, 16, n))


def unpack_weight(words, scales, fmt):
    g, _, n = scales.shape
    words = np.ascontiguousarray(words).reshape(g, 128, n, -1)
    if fmt == "e4m3":
        vals = words.view(ml_dtypes.float8_e4m3fn).astype(np.float64)
    else:
        nib = np.empty((g, 128, n, 4), np.uint8)
        nib[..., 0::2] = words & 0xF
        nib[..., 1::2] = words >> 4
        vals = E2M1[nib]
    vals = vals * np.repeat(np.exp2(scales.astype(np.float64) - 127.0), 8, axis=1)[..., None]
    return vals.transpose(0, 1, 3, 2).reshape(g * 512, n)


def gelu(v):
    return 0.5 * v * (1.0 + np.tanh(np.sqrt(2.0 / np.pi) * (v + 0.044715 * v**3)))


K, H, N, T, S = 1024, 512, 768, 2048, 512

def setup_inputs():
    n = np.random.standard_normal
    s = mx_kscale(K)[:, None]
    u = mx_kscale(H)[:, None]
    tab_words, tab_scales = pack_weight(n((K, T)) * s, "e4m3")
    w2_words, w2_scales = pack_weight(0.8 * n((K, H)) / np.sqrt(K) / s * u.T, "e2m1")
    w5_words, w5_scales = pack_weight(0.7 * n((K, N)) / np.sqrt(K) / s, "e2m1")
    return {
        "tab_words": tab_words, "tab_scales": tab_scales,
        "offs": striped(np.random.permutation(T)[:S]),
        "offs2": striped(np.random.permutation(T)[:S]),
        "offs3": striped(np.random.permutation(T)[:S]),
        "w1": (0.8 * n((K, H)) / np.sqrt(K) / s * u.T).astype(np.float32),
        "w2_words": w2_words, "w2_scales": w2_scales,
        "w3": (0.55 * n((K, H)) / np.sqrt(K) / s).astype(np.float32),
        "gain": (np.random.uniform(1.6, 2.8, H) * u[:, 0]).astype(np.float32),
        "w4": (n((H, N)) / np.sqrt(H) / u).astype(np.float32),
        "w5_words": w5_words, "w5_scales": w5_scales,
        "base": (0.5 * n(N)).astype(np.float32),
    }

def reference(tab_words, tab_scales, offs, offs2, offs3, w1, w2_words, w2_scales, w3, gain, w4, w5_words, w5_scales, base):
    TW = unpack_weight(tab_words, tab_scales, "e4m3")
    v = TW[:, unstriped(offs)]
    v2 = TW[:, unstriped(offs2)]
    v3 = TW[:, unstriped(offs3)]
    donor = mxq(f64(w1), 0, "e4m3").T @ v
    acceptor = unpack_weight(w2_words, w2_scales, "e2m1").T @ v2
    additive = mxq(f64(w3), 0, "e4m3").T @ v3
    h = np.maximum(donor, acceptor) + f64(gain)[:, None] * np.sin(additive)
    hq = mxq(h, 0, "e4m3")
    y = mxq(f64(w4), 0, "e4m3").T @ hq + unpack_weight(w5_words, w5_scales, "e2m1").T @ v
    return y + f64(base)[:, None]

@@ -1,0 +1,274 @@
+from contextlib import ExitStack
+
+import concourse.mybir as mybir
+
+K, H, N, T, S = 1024, 512, 768, 2048, 512
+FLOPS = 2 * S * (3 * K * H + H * N + K * N)
+
+F32 = mybir.dt.float32
+BF16 = mybir.dt.bfloat16
+I32 = mybir.dt.int32
+U32 = mybir.dt.uint32
+U16 = mybir.dt.uint16
+U8 = mybir.dt.uint8
+FP8X4 = mybir.dt.float8_e4m3fn_x4
+FP4X4 = mybir.dt.float4_e2m1fn_x4
+ACT = mybir.ActivationFunctionType
+ALU = mybir.AluOpType
+
+P = 128
+PACK = 4
+K_PASS = P * PACK
+PASSES = K // K_PASS
+QUADS = 4
+RUN = 4
+N_TILES = N // P
+W4_PARTS = 2
+W4_COLS = N // W4_PARTS
+HALVES = 2
+HALF = S // HALVES
+
+
+def tile_list_eutectic_melting_scores_kernel(
+    tc, tab_words, tab_scales, offs, offs2, offs3, w1, w2_words, w2_scales, w3, gain, w4, w5_words, w5_scales, base, out
+):
+    nc = tc.nc
+    with ExitStack() as ctx:
+        keep = ctx.enter_context(tc.tile_pool(name="keep", bufs=1))
+        ring = ctx.enter_context(tc.tile_pool(name="ring", bufs=2))
+        psum = ctx.enter_context(tc.psum_pool(name="psum", bufs=1))
+
+        def sb(name, shape, dtype, tag=""):
+            return keep.tile(shape, dtype, name=name, tag=tag or name, align_bytes=64)
+
+        def bank(b, name):
+            return psum.tile([P, S], F32, name=name, tag="bank%d" % b)
+
+        def copy_on(engine, dst, src):
+            if engine is nc.scalar:
+                nc.scalar.copy(dst, src)
+            else:
+                engine.tensor_copy(dst, src)
+
+        def load_rows(name, w, a):
+            raw = ring.tile([P, PACK, H], F32, name=name, tag="raw", align_bytes=64)
+            nc.sync.dma_start(raw[:], w[a * K_PASS : (a + 1) * K_PASS, :].rearrange("(p i) r -> p i r", i=PACK))
+            return raw
+
+        def load_table(a):
+            words = sb("tab_w%d" % a, [P, T], I32)
+            nc.sync.dma_start(words[:], tab_words[a].rearrange("p t i -> p (t i)").bitcast(I32))
+            return words
+
+        def load_weight_scales(queue, plane, scales):
+            for q in range(QUADS):
+                queue.dma_start(
+                    plane[32 * q : 32 * q + 4, :, :].bitcast(I32),
+                    scales[:, 4 * q : 4 * q + 4, :].rearrange("a r n -> r a n").bitcast(I32),
+                )
+
+        def gather_words(name, a):
+            picked = sb("v_%s%d" % (name, a), [P, S], U32)
+            nc.vector.tensor_copy(picked[:], tab_w[a][:].bitcast(U32).indirect(lists[name][:]))
+            v[name, a] = picked
+
+        def round_first_stage(engine, name, raw, t0, t1):
+            grouped = sb(name, [P, (t1 - t0) * P * PACK], BF16)
+            copy_on(
+                engine,
+                grouped[:].rearrange("p (t u e i) -> p t u i e", t=t1 - t0, e=RUN, i=PACK),
+                raw[:].rearrange("p i (u t e) -> p t u i e", t=PACK, e=RUN)[:, t0:t1],
+            )
+            return grouped
+
+        def interleave(engine, name, rows, width):
+            grouped = sb(name, [P, width * PACK], BF16)
+            copy_on(
+                engine,
+                grouped[:].rearrange("p (c e t) -> p c t e", e=RUN, t=PACK),
+                rows.rearrange("p t (c e) -> p c t e", e=RUN),
+            )
+            return grouped
+
+        def quantise(name, grouped, width):
+            codes = sb(name + "_codes", [P, width], U32)
+            scales = sb(name + "_scales", [P, width], U8)
+            nc.vector.quantize_mx(out=codes[:].bitcast(FP8X4), scales=scales[:], in_=grouped[:])
+            return codes, scales
+
+        lists = {}
+
+        def load_list(name, src):
+            lists[name] = keep.tile([P, S // 16], U16, name="list_" + name)
+            nc.sync.dma_start(lists[name][:], src)
+
+        load_list("acceptor", offs2)
+        load_list("donor", offs)
+
+        tab_sc = sb("tab_sc", [P, T], U8)
+        nc.vector.memset(tab_sc[:].bitcast(I32), 0)
+        w2_sc_raw = sb("w2_sc_raw", [P, PASSES, H], U8)
+        nc.vector.memset(w2_sc_raw[:].bitcast(I32), 0)
+        moved_sc = sb("moved_sc", [P, 2, S], U8)
+        nc.vector.memset(moved_sc[:].bitcast(I32), 0)
+        w5_sc = sb("w5_sc", [P, PASSES, N], U8)
+        nc.vector.memset(w5_sc[:].bitcast(I32), 0)
+        for q in range(QUADS):
+            nc.sync.dma_start(
+                tab_sc[32 * q : 32 * q + 4 * PASSES, :].bitcast(I32), tab_scales[:, 4 * q : 4 * q + 4, :].bitcast(I32)
+            )
+
+        w2_raw = sb("w2_raw", [P, PASSES, 2 * H], U8)
+        nc.sync.dma_start(w2_raw[:].bitcast(I32), w2_words.rearrange("a p n -> p a n").bitcast(I32))
+        tab_w = [load_table(0)]
+        load_list("additive", offs3)
+        load_weight_scales(nc.sync, w2_sc_raw, w2_scales)
+        w1_raw = [load_rows("w1_raw0", w1, 0)]
+        tab_w.append(load_table(1))
+        w1_raw.append(load_rows("w1_raw1", w1, 1))
+
+        v = {}
+        sc12 = sb("sc12", [P, 2, S], U8)
+        sc3 = sb("sc3", [P, S], U8)
+        nc.vector.tensor_copy(sc12[:, 0, :], tab_sc[:].indirect(lists["acceptor"][:]))
+        nc.vector.tensor_copy(sc12[:, 1, :], tab_sc[:].indirect(lists["donor"][:]))
+        for q in range(QUADS):
+            nc.sync.dma_start(
+                moved_sc[32 * q : 32 * q + 4, :, :].bitcast(I32), sc12[32 * q + 4 : 32 * q + 8, :, :].bitcast(I32)
+            )
+        gain_t = [sb("gain_t%d" % t, [P, 1], F32) for t in range(PACK)]
+        with nc.allow_non_contiguous_dma(reason="one value a partition"):
+            for t in range(PACK):
+                nc.gpsimd.dma_start(gain_t[t][:], gain.rearrange("(u t e) -> t u e", t=PACK, e=RUN)[t])
+            base_t = sb("base_t", [P, N_TILES], F32)
+            nc.gpsimd.dma_start(base_t[:], base.rearrange("(c p) -> p c", p=P))
+        load_weight_scales(nc.gpsimd, w5_sc, w5_scales)
+
+        w1_bf = [round_first_stage(nc.scalar, "w1_bf0", w1_raw[0], 0, PACK)]
+        w3_raw = [load_rows("w3_raw0", w3, 0)]
+        w1_bf.append(round_first_stage(nc.scalar, "w1_bf1", w1_raw[1], 0, PACK))
+        w3_raw.append(load_rows("w3_raw1", w3, 1))
+
+        w2_w = sb("w2_w", [P, PASSES, 2 * H], U8)
+        w2_sc = sb("w2_sc", [P, PASSES, H], U8)
+        nc.vector.tensor_copy(
+            w2_w[:].bitcast(I32).rearrange("p a (t u w) -> p a t u w", t=PACK, w=2),
+            w2_raw[:].bitcast(I32).rearrange("p a (u t w) -> p a t u w", t=PACK, w=2),
+        )
+        nc.vector.tensor_copy(sc3[:], tab_sc[:].indirect(lists["additive"][:]))
+        nc.vector.tensor_copy(
+            w2_sc[:].bitcast(I32).rearrange("p a (t u) -> p a t u", t=PACK),
+            w2_sc_raw[:].bitcast(I32).rearrange("p a (u t) -> p a t u", t=PACK),
+        )
+        for a in range(PASSES):
+            for name in ("acceptor", "donor", "additive"):
+                gather_words(name, a)
+        w1_q = [quantise("w1_%d" % a, w1_bf[a], H) for a in range(PASSES)]
+        w4_rows = w4.rearrange("(u t e) n -> t u e n", t=PACK, e=RUN)
+        w4_raw = sb("w4_raw", [P, W4_PARTS, PACK, W4_COLS], F32, tag="w1_bf1")
+        for c in range(W4_PARTS):
+            for t in range(PACK):
+                nc.sync.dma_start(w4_raw[:, c, t, :], w4_rows[t][:, :, c * W4_COLS : (c + 1) * W4_COLS])
+
+        v_sc = {
+            ("acceptor", 0): sc12[:, 0, :],
+            ("acceptor", 1): moved_sc[:, 0, :],
+            ("donor", 0): sc12[:, 1, :],
+            ("donor", 1): moved_sc[:, 1, :],
+            ("additive", 0): sc3[:],
+            ("additive", 1): sc3[4:P, :],
+        }
+
+        def product(acc, name, a, lhs, lhs_sc, cols, start, stop):
+            nc.tensor.matmul_mx(
+                out=acc, lhsT=lhs, lhsT_scale=lhs_sc, rhs=v[name, a][:, cols].bitcast(FP8X4),
+                rhs_scale=v_sc[name, a][:, cols], start=start, stop=stop,
+            )
+
+        every = slice(0, S)
+
+        acc_sb = []
+        for t in range(PACK):
+            acc = bank(t, "acceptor%d" % t)
+            for a in range(PASSES):
+                product(acc[:], "acceptor", a, w2_w[:, a, 2 * P * t : 2 * P * (t + 1)].bitcast(FP4X4),
+                        w2_sc[:, a, P * t : P * (t + 1)], every, a == 0, a == PASSES - 1)
+            held = sb("acceptor_sb%d" % t, [P, S], F32)
+            nc.scalar.copy(held[:], acc[:])
+            acc_sb.append(held)
+
+        w3_bf0 = round_first_stage(nc.scalar, "w3_bf0", w3_raw[0], 0, PACK)
+        w5_w = ring.tile([P, PASSES, 2 * N], U8, name="w5_w", tag="raw", align_bytes=64)
+        nc.sync.dma_start(w5_w[:].bitcast(I32), w5_words.rearrange("a p n -> p a n").bitcast(I32))
+        w4_bf0 = interleave(nc.scalar, "w4_bf0", w4_raw[:, 0], W4_COLS)
+
+        larger = []
+        for t in range(PACK):
+            acc = bank(PACK + t, "donor%d" % t)
+            for a in range(PASSES):
+                codes, scales = w1_q[a]
+                product(acc[:], "donor", a, codes[:, P * t : P * (t + 1)].bitcast(FP8X4),
+                        scales[:, P * t : P * (t + 1)], every, a == 0, a == PASSES - 1)
+            top = sb("larger%d" % t, [P, S], F32)
+            nc.vector.tensor_tensor(top[:], acc[:], acc_sb[t][:], ALU.max)
+            larger.append(top)
+
+        w3_bf1 = round_first_stage(nc.vector, "w3_bf1", w3_raw[1], 0, PACK)
+        w3_q = [quantise("w3_0", w3_bf0, H), quantise("w3_1", w3_bf1, H)]
+
+        additive = []
+        for t in range(PACK):
+            acc = bank(t, "additive%d" % t)
+            for a in range(PASSES):
+                codes, scales = w3_q[a]
+                product(acc[:], "additive", a, codes[:, P * t : P * (t + 1)].bitcast(FP8X4),
+                        scales[:, P * t : P * (t + 1)], every, a == 0, a == PASSES - 1)
+            additive.append(acc)
+
+        w4_bf1 = interleave(nc.vector, "w4_bf1", w4_raw[:, 1], W4_COLS)
+        w4_q = [quantise("w4_0", w4_bf0, W4_COLS)]
+
+        h32 = []
+        for half in range(HALVES):
+            cols = slice(half * HALF, (half + 1) * HALF)
+            rows = sb("h32_%d" % half, [P, PACK, HALF], F32)
+            for t in range(PACK):
+                wave = sb("wave%d_%d" % (half, t), [P, HALF], F32)
+                nc.scalar.activation(wave[:], additive[t][:, cols], ACT.Sin)
+                nc.vector.scalar_tensor_tensor(
+                    rows[:, t, :], wave[:], gain_t[t][:], larger[t][:, cols], ALU.mult, ALU.add
+                )
+            h32.append(rows)
+        h_bf0 = interleave(nc.scalar, "h_bf0", h32[0][:], HALF)
+        w4_q.append(quantise("w4_1", w4_bf1, W4_COLS))
+        h_bf1 = interleave(nc.vector, "h_bf1", h32[1][:], HALF)
+        h_q = [quantise("h0", h_bf0, HALF), quantise("h1", h_bf1, HALF)]
+
+        pairs = N_TILES // 2
+        for half in range(HALVES):
+            cols = slice(half * HALF, (half + 1) * HALF)
+            h_codes, h_scales = h_q[half]
+            for pair in range(pairs):
+                acc = bank((PACK + half * pairs + pair) % 8, "score%d_%d" % (half, pair))
+                tiles = [(2 * pair + side, acc[:, side * HALF : (side + 1) * HALF]) for side in range(2)]
+                for m, part in tiles:
+                    for a in range(PASSES):
+                        product(part, "donor", a, w5_w[:, a, 2 * P * m : 2 * P * (m + 1)].bitcast(FP4X4),
+                                w5_sc[:, a, P * m : P * (m + 1)], cols, m % 2 == 0 and a == 0, False)
+                for m, part in tiles:
+                    c, first = divmod(m * P, W4_COLS)
+                    codes, scales = w4_q[c]
+                    nc.tensor.matmul_mx(
+                        out=part, lhsT=codes[:, first : first + P].bitcast(FP8X4),
+                        lhsT_scale=scales[:, first : first + P], rhs=h_codes[:].bitcast(FP8X4),
+                        rhs_scale=h_scales[:], start=False, stop=m % 2 == 1,
+                    )
+                result = sb("result%d_%d" % (half, pair), [P, 2, HALF], F32)
+                for m, part in tiles:
+                    if half == 0 or pair == 1:
+                        nc.scalar.activation(result[:, m % 2, :], part, ACT.Identity, bias=base_t[:, m : m + 1])
+                    else:
+                        nc.vector.tensor_scalar_add(result[:, m % 2, :], part, base_t[:, m : m + 1])
+                nc.sync.dma_start(
+                    out[2 * pair * P : 2 * (pair + 1) * P, cols].rearrange("(m p) j -> p m j", p=P), result[:]
+                )

@@ -25,8 +25,7 @@ RUN = 4
 N_TILES = N // P
 W4_PARTS = 2
 W4_COLS = N // W4_PARTS
-HALVES = 2
-HALF = S // HALVES
+H_SPLIT = 352
 
 
 def tile_list_eutectic_melting_scores_kernel(
@@ -35,11 +34,14 @@ def tile_list_eutectic_melting_scores_kernel(
     nc = tc.nc
     with ExitStack() as ctx:
         keep = ctx.enter_context(tc.tile_pool(name="keep", bufs=1))
-        ring = ctx.enter_context(tc.tile_pool(name="ring", bufs=2))
+        reuse = ctx.enter_context(tc.tile_pool(name="reuse", bufs=1))
         psum = ctx.enter_context(tc.psum_pool(name="psum", bufs=1))
 
         def sb(name, shape, dtype, tag=""):
             return keep.tile(shape, dtype, name=name, tag=tag or name, align_bytes=64)
+
+        def placed(name, shape, dtype, offset):
+            return reuse.tile(shape, dtype, name=name, align_bytes=64, offset=offset)
 
         def bank(b, name):
             return psum.tile([P, S], F32, name=name, tag="bank%d" % b)
@@ -50,8 +52,7 @@ def tile_list_eutectic_melting_scores_kernel(
             else:
                 engine.tensor_copy(dst, src)
 
-        def load_rows(name, w, a):
-            raw = ring.tile([P, PACK, H], F32, name=name, tag="raw", align_bytes=64)
+        def load_rows(raw, w, a):
             nc.sync.dma_start(raw[:], w[a * K_PASS : (a + 1) * K_PASS, :].rearrange("(p i) r -> p i r", i=PACK))
             return raw
 
@@ -81,14 +82,12 @@ def tile_list_eutectic_melting_scores_kernel(
             )
             return grouped
 
-        def interleave(engine, name, rows, width):
-            grouped = sb(name, [P, width * PACK], BF16)
+        def interleave(engine, grouped, rows):
             copy_on(
                 engine,
-                grouped[:].rearrange("p (c e t) -> p c t e", e=RUN, t=PACK),
+                grouped.rearrange("p (c e t) -> p c t e", e=RUN, t=PACK),
                 rows.rearrange("p t (c e) -> p c t e", e=RUN),
             )
-            return grouped
 
         def quantise(name, grouped, width):
             codes = sb(name + "_codes", [P, width], U32)
@@ -111,21 +110,23 @@ def tile_list_eutectic_melting_scores_kernel(
         nc.vector.memset(w2_sc_raw[:].bitcast(I32), 0)
         moved_sc = sb("moved_sc", [P, 2, S], U8)
         nc.vector.memset(moved_sc[:].bitcast(I32), 0)
-        w5_sc = sb("w5_sc", [P, PASSES, N], U8)
-        nc.vector.memset(w5_sc[:].bitcast(I32), 0)
         for q in range(QUADS):
             nc.sync.dma_start(
                 tab_sc[32 * q : 32 * q + 4 * PASSES, :].bitcast(I32), tab_scales[:, 4 * q : 4 * q + 4, :].bitcast(I32)
             )
 
+        w5_sc = sb("w5_sc", [P, PASSES, N], U8)
+        nc.gpsimd.memset(w5_sc[:].bitcast(I32), 0)
+        load_weight_scales(nc.gpsimd, w5_sc, w5_scales)
+
         w2_raw = sb("w2_raw", [P, PASSES, 2 * H], U8)
         nc.sync.dma_start(w2_raw[:].bitcast(I32), w2_words.rearrange("a p n -> p a n").bitcast(I32))
         tab_w = [load_table(0)]
         load_list("additive", offs3)
+        w1_raw = [load_rows(placed("w1_raw0", [P, PACK, H], F32, 11264), w1, 0)]
         load_weight_scales(nc.sync, w2_sc_raw, w2_scales)
-        w1_raw = [load_rows("w1_raw0", w1, 0)]
         tab_w.append(load_table(1))
-        w1_raw.append(load_rows("w1_raw1", w1, 1))
+        w1_raw.append(load_rows(sb("w1_raw1", [P, PACK, H], F32), w1, 1))
 
         v = {}
         sc12 = sb("sc12", [P, 2, S], U8)
@@ -136,18 +137,8 @@ def tile_list_eutectic_melting_scores_kernel(
             nc.sync.dma_start(
                 moved_sc[32 * q : 32 * q + 4, :, :].bitcast(I32), sc12[32 * q + 4 : 32 * q + 8, :, :].bitcast(I32)
             )
-        gain_t = [sb("gain_t%d" % t, [P, 1], F32) for t in range(PACK)]
-        with nc.allow_non_contiguous_dma(reason="one value a partition"):
-            for t in range(PACK):
-                nc.gpsimd.dma_start(gain_t[t][:], gain.rearrange("(u t e) -> t u e", t=PACK, e=RUN)[t])
-            base_t = sb("base_t", [P, N_TILES], F32)
-            nc.gpsimd.dma_start(base_t[:], base.rearrange("(c p) -> p c", p=P))
-        load_weight_scales(nc.gpsimd, w5_sc, w5_scales)
 
-        w1_bf = [round_first_stage(nc.scalar, "w1_bf0", w1_raw[0], 0, PACK)]
-        w3_raw = [load_rows("w3_raw0", w3, 0)]
-        w1_bf.append(round_first_stage(nc.scalar, "w1_bf1", w1_raw[1], 0, PACK))
-        w3_raw.append(load_rows("w3_raw1", w3, 1))
+        w1_bf = [round_first_stage(nc.scalar, "w1_bf%d" % a, w1_raw[a], 0, PACK) for a in range(PASSES)]
 
         w2_w = sb("w2_w", [P, PASSES, 2 * H], U8)
         w2_sc = sb("w2_sc", [P, PASSES, H], U8)
@@ -156,6 +147,24 @@ def tile_list_eutectic_melting_scores_kernel(
             w2_raw[:].bitcast(I32).rearrange("p a (u t w) -> p a t u w", t=PACK, w=2),
         )
         nc.vector.tensor_copy(sc3[:], tab_sc[:].indirect(lists["additive"][:]))
+        w3_raw = [
+            load_rows(sb("w3_raw0", [P, PACK, H], F32, "tab_sc"), w3, 0),
+            load_rows(placed("w3_raw1", [P, PACK, H], F32, 18432), w3, 1),
+        ]
+        base_t = placed("base_t", [P, N_TILES], F32, 15360)
+        w5_w = placed("w5_w", [P, PASSES, 2 * N], U8, 12288)
+        gain_t = [placed("gain_t%d" % t, [P, 1], F32, 15424 + 64 * t) for t in range(PACK)]
+        with nc.allow_non_contiguous_dma(reason="one value a partition and tile"):
+            nc.sync.dma_start(base_t[:], base.rearrange("(c p) -> p c", p=P))
+            nc.sync.dma_start(w5_w[:].bitcast(I32), w5_words.rearrange("a p n -> p a n").bitcast(I32))
+        w4_rows = w4.rearrange("(u t e) n -> t u e n", t=PACK, e=RUN)
+        w4_raw = placed("w4_raw", [P, W4_PARTS, PACK, W4_COLS], F32, 0)
+        for c in range(W4_PARTS):
+            for t in range(PACK):
+                nc.sync.dma_start(w4_raw[:, c, t, :], w4_rows[t][:, :, c * W4_COLS : (c + 1) * W4_COLS])
+        with nc.allow_non_contiguous_dma(reason="one value a partition"):
+            for t in range(PACK):
+                nc.sync.dma_start(gain_t[t][:], gain.rearrange("(u t e) -> t u e", t=PACK, e=RUN)[t])
         nc.vector.tensor_copy(
             w2_sc[:].bitcast(I32).rearrange("p a (t u) -> p a t u", t=PACK),
             w2_sc_raw[:].bitcast(I32).rearrange("p a (u t) -> p a t u", t=PACK),
@@ -164,11 +173,6 @@ def tile_list_eutectic_melting_scores_kernel(
             for name in ("acceptor", "donor", "additive"):
                 gather_words(name, a)
         w1_q = [quantise("w1_%d" % a, w1_bf[a], H) for a in range(PASSES)]
-        w4_rows = w4.rearrange("(u t e) n -> t u e n", t=PACK, e=RUN)
-        w4_raw = sb("w4_raw", [P, W4_PARTS, PACK, W4_COLS], F32, tag="w1_bf1")
-        for c in range(W4_PARTS):
-            for t in range(PACK):
-                nc.sync.dma_start(w4_raw[:, c, t, :], w4_rows[t][:, :, c * W4_COLS : (c + 1) * W4_COLS])
 
         v_sc = {
             ("acceptor", 0): sc12[:, 0, :],
@@ -179,96 +183,90 @@ def tile_list_eutectic_melting_scores_kernel(
             ("additive", 1): sc3[4:P, :],
         }
 
-        def product(acc, name, a, lhs, lhs_sc, cols, start, stop):
+        def product(acc, name, a, lhs, lhs_sc, start, stop):
             nc.tensor.matmul_mx(
-                out=acc, lhsT=lhs, lhsT_scale=lhs_sc, rhs=v[name, a][:, cols].bitcast(FP8X4),
-                rhs_scale=v_sc[name, a][:, cols], start=start, stop=stop,
+                out=acc, lhsT=lhs, lhsT_scale=lhs_sc, rhs=v[name, a][:].bitcast(FP8X4),
+                rhs_scale=v_sc[name, a], start=start, stop=stop,
             )
 
-        every = slice(0, S)
 
+        acceptor = [bank(t, "acceptor%d" % t) for t in range(PACK)]
         acc_sb = []
+        for a in range(PASSES):
+            for t in range(PACK):
+                product(acceptor[t][:], "acceptor", a, w2_w[:, a, 2 * P * t : 2 * P * (t + 1)].bitcast(FP4X4),
+                        w2_sc[:, a, P * t : P * (t + 1)], a == 0, a == PASSES - 1)
         for t in range(PACK):
-            acc = bank(t, "acceptor%d" % t)
-            for a in range(PASSES):
-                product(acc[:], "acceptor", a, w2_w[:, a, 2 * P * t : 2 * P * (t + 1)].bitcast(FP4X4),
-                        w2_sc[:, a, P * t : P * (t + 1)], every, a == 0, a == PASSES - 1)
             held = sb("acceptor_sb%d" % t, [P, S], F32)
-            nc.scalar.copy(held[:], acc[:])
+            nc.scalar.copy(held[:], acceptor[t][:])
             acc_sb.append(held)
 
         w3_bf0 = round_first_stage(nc.scalar, "w3_bf0", w3_raw[0], 0, PACK)
-        w5_w = ring.tile([P, PASSES, 2 * N], U8, name="w5_w", tag="raw", align_bytes=64)
-        nc.sync.dma_start(w5_w[:].bitcast(I32), w5_words.rearrange("a p n -> p a n").bitcast(I32))
-        w4_bf0 = interleave(nc.scalar, "w4_bf0", w4_raw[:, 0], W4_COLS)
+        w4_bf0 = sb("w4_bf0", [P, W4_COLS * PACK], BF16, "tab_sc")
+        interleave(nc.scalar, w4_bf0[:], w4_raw[:, 0])
 
+        donor = [bank(PACK + t, "donor%d" % t) for t in range(PACK)]
+        for a in range(PASSES):
+            codes, scales = w1_q[a]
+            for t in range(PACK):
+                product(donor[t][:], "donor", a, codes[:, P * t : P * (t + 1)].bitcast(FP8X4),
+                        scales[:, P * t : P * (t + 1)], a == 0, a == PASSES - 1)
         larger = []
         for t in range(PACK):
-            acc = bank(PACK + t, "donor%d" % t)
-            for a in range(PASSES):
-                codes, scales = w1_q[a]
-                product(acc[:], "donor", a, codes[:, P * t : P * (t + 1)].bitcast(FP8X4),
-                        scales[:, P * t : P * (t + 1)], every, a == 0, a == PASSES - 1)
             top = sb("larger%d" % t, [P, S], F32)
-            nc.vector.tensor_tensor(top[:], acc[:], acc_sb[t][:], ALU.max)
+            nc.vector.tensor_tensor(top[:], donor[t][:], acc_sb[t][:], ALU.max)
             larger.append(top)
 
         w3_bf1 = round_first_stage(nc.vector, "w3_bf1", w3_raw[1], 0, PACK)
-        w3_q = [quantise("w3_0", w3_bf0, H), quantise("w3_1", w3_bf1, H)]
+        w3_q = {1: quantise("w3_1", w3_bf1, H), 0: quantise("w3_0", w3_bf0, H)}
 
-        additive = []
-        for t in range(PACK):
-            acc = bank(t, "additive%d" % t)
+        scores = []
+
+        def open_scores(m):
+            acc = bank(m, "score%d" % m)
             for a in range(PASSES):
-                codes, scales = w3_q[a]
-                product(acc[:], "additive", a, codes[:, P * t : P * (t + 1)].bitcast(FP8X4),
-                        scales[:, P * t : P * (t + 1)], every, a == 0, a == PASSES - 1)
-            additive.append(acc)
+                product(acc[:], "donor", a, w5_w[:, a, 2 * P * m : 2 * P * (m + 1)].bitcast(FP4X4),
+                        w5_sc[:, a, P * m : P * (m + 1)], a == 0, False)
+            scores.append(acc)
 
-        w4_bf1 = interleave(nc.vector, "w4_bf1", w4_raw[:, 1], W4_COLS)
-        w4_q = [quantise("w4_0", w4_bf0, W4_COLS)]
+        for m in range(PACK):
+            open_scores(m)
 
-        h32 = []
-        for half in range(HALVES):
-            cols = slice(half * HALF, (half + 1) * HALF)
-            rows = sb("h32_%d" % half, [P, PACK, HALF], F32)
+        additive = [bank(PACK + t, "additive%d" % t) for t in range(PACK)]
+        for a in (1, 0):
+            codes, scales = w3_q[a]
             for t in range(PACK):
-                wave = sb("wave%d_%d" % (half, t), [P, HALF], F32)
-                nc.scalar.activation(wave[:], additive[t][:, cols], ACT.Sin)
-                nc.vector.scalar_tensor_tensor(
-                    rows[:, t, :], wave[:], gain_t[t][:], larger[t][:, cols], ALU.mult, ALU.add
-                )
-            h32.append(rows)
-        h_bf0 = interleave(nc.scalar, "h_bf0", h32[0][:], HALF)
-        w4_q.append(quantise("w4_1", w4_bf1, W4_COLS))
-        h_bf1 = interleave(nc.vector, "h_bf1", h32[1][:], HALF)
-        h_q = [quantise("h0", h_bf0, HALF), quantise("h1", h_bf1, HALF)]
+                product(additive[t][:], "additive", a, codes[:, P * t : P * (t + 1)].bitcast(FP8X4),
+                        scales[:, P * t : P * (t + 1)], a == 1, a == 0)
 
-        pairs = N_TILES // 2
-        for half in range(HALVES):
-            cols = slice(half * HALF, (half + 1) * HALF)
-            h_codes, h_scales = h_q[half]
-            for pair in range(pairs):
-                acc = bank((PACK + half * pairs + pair) % 8, "score%d_%d" % (half, pair))
-                tiles = [(2 * pair + side, acc[:, side * HALF : (side + 1) * HALF]) for side in range(2)]
-                for m, part in tiles:
-                    for a in range(PASSES):
-                        product(part, "donor", a, w5_w[:, a, 2 * P * m : 2 * P * (m + 1)].bitcast(FP4X4),
-                                w5_sc[:, a, P * m : P * (m + 1)], cols, m % 2 == 0 and a == 0, False)
-                for m, part in tiles:
-                    c, first = divmod(m * P, W4_COLS)
-                    codes, scales = w4_q[c]
-                    nc.tensor.matmul_mx(
-                        out=part, lhsT=codes[:, first : first + P].bitcast(FP8X4),
-                        lhsT_scale=scales[:, first : first + P], rhs=h_codes[:].bitcast(FP8X4),
-                        rhs_scale=h_scales[:], start=False, stop=m % 2 == 1,
-                    )
-                result = sb("result%d_%d" % (half, pair), [P, 2, HALF], F32)
-                for m, part in tiles:
-                    if half == 0 or pair == 1:
-                        nc.scalar.activation(result[:, m % 2, :], part, ACT.Identity, bias=base_t[:, m : m + 1])
-                    else:
-                        nc.vector.tensor_scalar_add(result[:, m % 2, :], part, base_t[:, m : m + 1])
-                nc.sync.dma_start(
-                    out[2 * pair * P : 2 * (pair + 1) * P, cols].rearrange("(m p) j -> p m j", p=P), result[:]
-                )
+        w4_bf1 = sb("w4_bf1", [P, W4_COLS * PACK], BF16, "w3_bf0")
+        interleave(nc.vector, w4_bf1[:], w4_raw[:, 1])
+        w4_q = [quantise("w4_0", w4_bf0, W4_COLS), quantise("w4_1", w4_bf1, W4_COLS)]
+
+        h32 = sb("h32", [P, PACK, S], F32)
+        for t in range(PACK):
+            wave = sb("wave%d" % t, [P, S], F32)
+            nc.scalar.activation(wave[:], additive[t][:], ACT.Sin)
+            nc.vector.scalar_tensor_tensor(h32[:, t, :], wave[:], gain_t[t][:], larger[t][:], ALU.mult, ALU.add)
+        for m in range(PACK, N_TILES):
+            open_scores(m)
+        h_bf = sb("h_bf", [P, S * PACK], BF16)
+        interleave(nc.vector, h_bf[:, : H_SPLIT * PACK], h32[:, :, :H_SPLIT])
+        interleave(nc.scalar, h_bf[:, H_SPLIT * PACK :], h32[:, :, H_SPLIT:])
+        h_codes, h_scales = quantise("h", h_bf, S)
+
+        for m in range(N_TILES):
+            c, first = divmod(m * P, W4_COLS)
+            codes, scales = w4_q[c]
+            nc.tensor.matmul_mx(
+                out=scores[m][:], lhsT=codes[:, first : first + P].bitcast(FP8X4),
+                lhsT_scale=scales[:, first : first + P], rhs=h_codes[:].bitcast(FP8X4),
+                rhs_scale=h_scales[:], start=False, stop=True,
+            )
+        for m in range(N_TILES):
+            result = sb("result%d" % m, [P, S], F32)
+            if m % 2 == 0:
+                nc.scalar.activation(result[:], scores[m][:], ACT.Identity, bias=base_t[:, m : m + 1])
+            else:
+                nc.vector.tensor_scalar_add(result[:], scores[m][:], base_t[:, m : m + 1])
+            nc.sync.dma_start(out[m * P : (m + 1) * P, :], result[:])

@@ -73,14 +73,12 @@ def tile_list_eutectic_melting_scores_kernel(
             nc.vector.tensor_copy(picked[:], tab_w[a][:].bitcast(U32).indirect(lists[name][:]))
             v[name, a] = picked
 
-        def round_first_stage(engine, name, raw, t0, t1):
-            grouped = sb(name, [P, (t1 - t0) * P * PACK], BF16)
+        def round_first_stage(engine, grouped, raw, t0, t1):
             copy_on(
                 engine,
-                grouped[:].rearrange("p (t u e i) -> p t u i e", t=t1 - t0, e=RUN, i=PACK),
+                grouped[:].rearrange("p (t u e i) -> p t u i e", t=PACK, e=RUN, i=PACK)[:, t0:t1],
                 raw[:].rearrange("p i (u t e) -> p t u i e", t=PACK, e=RUN)[:, t0:t1],
             )
-            return grouped
 
         def interleave(engine, grouped, rows):
             copy_on(
@@ -103,6 +101,7 @@ def tile_list_eutectic_melting_scores_kernel(
 
         load_list("acceptor", offs2)
         load_list("donor", offs)
+        load_list("additive", offs3)
 
         tab_sc = sb("tab_sc", [P, T], U8)
         nc.vector.memset(tab_sc[:].bitcast(I32), 0)
@@ -119,14 +118,13 @@ def tile_list_eutectic_melting_scores_kernel(
         nc.gpsimd.memset(w5_sc[:].bitcast(I32), 0)
         load_weight_scales(nc.gpsimd, w5_sc, w5_scales)
 
+        tab_w = [load_table(0)]
         w2_raw = sb("w2_raw", [P, PASSES, 2 * H], U8)
         nc.sync.dma_start(w2_raw[:].bitcast(I32), w2_words.rearrange("a p n -> p a n").bitcast(I32))
-        tab_w = [load_table(0)]
-        load_list("additive", offs3)
-        w1_raw = [load_rows(placed("w1_raw0", [P, PACK, H], F32, 11264), w1, 0)]
+        w1_raw = [load_rows(placed("w1_raw0", [P, PACK, H], F32, 7168), w1, 0)]
         load_weight_scales(nc.sync, w2_sc_raw, w2_scales)
         tab_w.append(load_table(1))
-        w1_raw.append(load_rows(sb("w1_raw1", [P, PACK, H], F32), w1, 1))
+        w1_raw.append(load_rows(placed("w1_raw1", [P, PACK, H], F32, 22528), w1, 1))
 
         v = {}
         sc12 = sb("sc12", [P, 2, S], U8)
@@ -138,27 +136,27 @@ def tile_list_eutectic_melting_scores_kernel(
                 moved_sc[32 * q : 32 * q + 4, :, :].bitcast(I32), sc12[32 * q + 4 : 32 * q + 8, :, :].bitcast(I32)
             )
 
-        w1_bf = [round_first_stage(nc.scalar, "w1_bf%d" % a, w1_raw[a], 0, PACK) for a in range(PASSES)]
+        w1_bf = [sb("w1_bf%d" % a, [P, H * PACK], BF16) for a in range(PASSES)]
+        round_first_stage(nc.scalar, w1_bf[0], w1_raw[0], 0, PACK)
+        round_first_stage(nc.scalar, w1_bf[1], w1_raw[1], 0, PACK // 2)
 
-        w2_w = sb("w2_w", [P, PASSES, 2 * H], U8)
+        nc.vector.tensor_copy(sc3[:], tab_sc[:].indirect(lists["additive"][:]))
+        w2_w = sb("w2_w", [P, PASSES, 2 * H], U8, "tab_sc")
         w2_sc = sb("w2_sc", [P, PASSES, H], U8)
         nc.vector.tensor_copy(
             w2_w[:].bitcast(I32).rearrange("p a (t u w) -> p a t u w", t=PACK, w=2),
             w2_raw[:].bitcast(I32).rearrange("p a (u t w) -> p a t u w", t=PACK, w=2),
         )
-        nc.vector.tensor_copy(sc3[:], tab_sc[:].indirect(lists["additive"][:]))
         w3_raw = [
-            load_rows(sb("w3_raw0", [P, PACK, H], F32, "tab_sc"), w3, 0),
-            load_rows(placed("w3_raw1", [P, PACK, H], F32, 18432), w3, 1),
+            load_rows(placed("w3_raw0", [P, PACK, H], F32, 0), w3, 0),
+            load_rows(placed("w3_raw1", [P, PACK, H], F32, 14336), w3, 1),
         ]
-        base_t = placed("base_t", [P, N_TILES], F32, 15360)
-        w5_w = placed("w5_w", [P, PASSES, 2 * N], U8, 12288)
-        gain_t = [placed("gain_t%d" % t, [P, 1], F32, 15424 + 64 * t) for t in range(PACK)]
+        base_t = placed("base_t", [P, N_TILES], F32, 11264)
+        gain_t = [placed("gain_t%d" % t, [P, 1], F32, 22528 + 64 * t) for t in range(PACK)]
         with nc.allow_non_contiguous_dma(reason="one value a partition and tile"):
             nc.sync.dma_start(base_t[:], base.rearrange("(c p) -> p c", p=P))
-            nc.sync.dma_start(w5_w[:].bitcast(I32), w5_words.rearrange("a p n -> p a n").bitcast(I32))
         w4_rows = w4.rearrange("(u t e) n -> t u e n", t=PACK, e=RUN)
-        w4_raw = placed("w4_raw", [P, W4_PARTS, PACK, W4_COLS], F32, 0)
+        w4_raw = placed("w4_raw", [P, W4_PARTS, PACK, W4_COLS], F32, 23552)
         for c in range(W4_PARTS):
             for t in range(PACK):
                 nc.sync.dma_start(w4_raw[:, c, t, :], w4_rows[t][:, :, c * W4_COLS : (c + 1) * W4_COLS])
@@ -172,6 +170,7 @@ def tile_list_eutectic_melting_scores_kernel(
         for a in range(PASSES):
             for name in ("acceptor", "donor", "additive"):
                 gather_words(name, a)
+        round_first_stage(nc.vector, w1_bf[1], w1_raw[1], PACK // 2, PACK)
         w1_q = [quantise("w1_%d" % a, w1_bf[a], H) for a in range(PASSES)]
 
         v_sc = {
@@ -201,8 +200,11 @@ def tile_list_eutectic_melting_scores_kernel(
             nc.scalar.copy(held[:], acceptor[t][:])
             acc_sb.append(held)
 
-        w3_bf0 = round_first_stage(nc.scalar, "w3_bf0", w3_raw[0], 0, PACK)
-        w4_bf0 = sb("w4_bf0", [P, W4_COLS * PACK], BF16, "tab_sc")
+        w3_bf0 = sb("w3_bf0", [P, H * PACK], BF16)
+        round_first_stage(nc.scalar, w3_bf0, w3_raw[0], 0, PACK)
+        w5_w = placed("w5_w", [P, PASSES, 2 * N], U8, 3072)
+        nc.sync.dma_start(w5_w[:].bitcast(I32), w5_words.rearrange("a p n -> p a n").bitcast(I32))
+        w4_bf0 = placed("w4_bf0", [P, W4_COLS * PACK], BF16, 0)
         interleave(nc.scalar, w4_bf0[:], w4_raw[:, 0])
 
         donor = [bank(PACK + t, "donor%d" % t) for t in range(PACK)]
@@ -217,7 +219,8 @@ def tile_list_eutectic_melting_scores_kernel(
             nc.vector.tensor_tensor(top[:], donor[t][:], acc_sb[t][:], ALU.max)
             larger.append(top)
 
-        w3_bf1 = round_first_stage(nc.vector, "w3_bf1", w3_raw[1], 0, PACK)
+        w3_bf1 = sb("w3_bf1", [P, H * PACK], BF16)
+        round_first_stage(nc.vector, w3_bf1, w3_raw[1], 0, PACK)
         w3_q = {1: quantise("w3_1", w3_bf1, H), 0: quantise("w3_0", w3_bf0, H)}
 
         scores = []
@@ -229,31 +232,30 @@ def tile_list_eutectic_melting_scores_kernel(
                         w5_sc[:, a, P * m : P * (m + 1)], a == 0, False)
             scores.append(acc)
 
-        for m in range(PACK):
-            open_scores(m)
-
         additive = [bank(PACK + t, "additive%d" % t) for t in range(PACK)]
-        for a in (1, 0):
-            codes, scales = w3_q[a]
-            for t in range(PACK):
-                product(additive[t][:], "additive", a, codes[:, P * t : P * (t + 1)].bitcast(FP8X4),
-                        scales[:, P * t : P * (t + 1)], a == 1, a == 0)
+        for first in range(0, PACK, 2):
+            for a in (1, 0):
+                codes, scales = w3_q[a]
+                for t in (first, first + 1):
+                    product(additive[t][:], "additive", a, codes[:, P * t : P * (t + 1)].bitcast(FP8X4),
+                            scales[:, P * t : P * (t + 1)], a == 1, a == 0)
 
         w4_bf1 = sb("w4_bf1", [P, W4_COLS * PACK], BF16, "w3_bf0")
         interleave(nc.vector, w4_bf1[:], w4_raw[:, 1])
-        w4_q = [quantise("w4_0", w4_bf0, W4_COLS), quantise("w4_1", w4_bf1, W4_COLS)]
+        w4_q = [quantise("w4_0", w4_bf0, W4_COLS)]
 
         h32 = sb("h32", [P, PACK, S], F32)
         for t in range(PACK):
             wave = sb("wave%d" % t, [P, S], F32)
             nc.scalar.activation(wave[:], additive[t][:], ACT.Sin)
             nc.vector.scalar_tensor_tensor(h32[:, t, :], wave[:], gain_t[t][:], larger[t][:], ALU.mult, ALU.add)
-        for m in range(PACK, N_TILES):
+        for m in range(N_TILES):
             open_scores(m)
         h_bf = sb("h_bf", [P, S * PACK], BF16)
         interleave(nc.vector, h_bf[:, : H_SPLIT * PACK], h32[:, :, :H_SPLIT])
         interleave(nc.scalar, h_bf[:, H_SPLIT * PACK :], h32[:, :, H_SPLIT:])
         h_codes, h_scales = quantise("h", h_bf, S)
+        w4_q.append(quantise("w4_1", w4_bf1, W4_COLS))
 
         for m in range(N_TILES):
             c, first = divmod(m * P, W4_COLS)

from contextlib import ExitStack

import concourse.mybir as mybir

K, H, N, T, S = 1024, 512, 768, 2048, 512
FLOPS = 2 * S * (3 * K * H + H * N + K * N)

F32 = mybir.dt.float32
BF16 = mybir.dt.bfloat16
I32 = mybir.dt.int32
U32 = mybir.dt.uint32
U16 = mybir.dt.uint16
U8 = mybir.dt.uint8
FP8X4 = mybir.dt.float8_e4m3fn_x4
FP4X4 = mybir.dt.float4_e2m1fn_x4
ACT = mybir.ActivationFunctionType
ALU = mybir.AluOpType

P = 128
PACK = 4
K_PASS = P * PACK
PASSES = K // K_PASS
QUADS = 4
RUN = 4
N_TILES = N // P
W4_PARTS = 2
W4_COLS = N // W4_PARTS
H_SPLIT = 352


def tile_list_eutectic_melting_scores_kernel(
    tc, tab_words, tab_scales, offs, offs2, offs3, w1, w2_words, w2_scales, w3, gain, w4, w5_words, w5_scales, base, out
):
    nc = tc.nc
    with ExitStack() as ctx:
        keep = ctx.enter_context(tc.tile_pool(name="keep", bufs=1))
        reuse = ctx.enter_context(tc.tile_pool(name="reuse", bufs=1))
        psum = ctx.enter_context(tc.psum_pool(name="psum", bufs=1))

        def sb(name, shape, dtype, tag=""):
            return keep.tile(shape, dtype, name=name, tag=tag or name, align_bytes=64)

        def placed(name, shape, dtype, offset):
            return reuse.tile(shape, dtype, name=name, align_bytes=64, offset=offset)

        def bank(b, name):
            return psum.tile([P, S], F32, name=name, tag="bank%d" % b)

        def copy_on(engine, dst, src):
            if engine is nc.scalar:
                nc.scalar.copy(dst, src)
            else:
                engine.tensor_copy(dst, src)

        def load_rows(raw, w, a):
            nc.sync.dma_start(raw[:], w[a * K_PASS : (a + 1) * K_PASS, :].rearrange("(p i) r -> p i r", i=PACK))
            return raw

        def load_table(a):
            words = sb("tab_w%d" % a, [P, T], I32)
            nc.sync.dma_start(words[:], tab_words[a].rearrange("p t i -> p (t i)").bitcast(I32))
            return words

        def load_weight_scales(queue, plane, scales):
            for q in range(QUADS):
                queue.dma_start(
                    plane[32 * q : 32 * q + 4, :, :].bitcast(I32),
                    scales[:, 4 * q : 4 * q + 4, :].rearrange("a r n -> r a n").bitcast(I32),
                )

        def gather_words(name, a):
            picked = sb("v_%s%d" % (name, a), [P, S], U32)
            nc.vector.tensor_copy(picked[:], tab_w[a][:].bitcast(U32).indirect(lists[name][:]))
            v[name, a] = picked

        def round_first_stage(engine, grouped, raw, t0, t1):
            copy_on(
                engine,
                grouped[:].rearrange("p (t u e i) -> p t u i e", t=PACK, e=RUN, i=PACK)[:, t0:t1],
                raw[:].rearrange("p i (u t e) -> p t u i e", t=PACK, e=RUN)[:, t0:t1],
            )

        def interleave(engine, grouped, rows):
            copy_on(
                engine,
                grouped.rearrange("p (c e t) -> p c t e", e=RUN, t=PACK),
                rows.rearrange("p t (c e) -> p c t e", e=RUN),
            )

        def quantise(name, grouped, width):
            codes = sb(name + "_codes", [P, width], U32)
            scales = sb(name + "_scales", [P, width], U8)
            nc.vector.quantize_mx(out=codes[:].bitcast(FP8X4), scales=scales[:], in_=grouped[:])
            return codes, scales

        lists = {}

        def load_list(name, src):
            lists[name] = keep.tile([P, S // 16], U16, name="list_" + name)
            nc.sync.dma_start(lists[name][:], src)

        load_list("acceptor", offs2)
        load_list("donor", offs)
        load_list("additive", offs3)

        tab_sc = sb("tab_sc", [P, T], U8)
        nc.vector.memset(tab_sc[:].bitcast(I32), 0)
        w2_sc_raw = sb("w2_sc_raw", [P, PASSES, H], U8)
        nc.vector.memset(w2_sc_raw[:].bitcast(I32), 0)
        moved_sc = sb("moved_sc", [P, 2, S], U8)
        nc.vector.memset(moved_sc[:].bitcast(I32), 0)
        for q in range(QUADS):
            nc.sync.dma_start(
                tab_sc[32 * q : 32 * q + 4 * PASSES, :].bitcast(I32), tab_scales[:, 4 * q : 4 * q + 4, :].bitcast(I32)
            )

        w5_sc = sb("w5_sc", [P, PASSES, N], U8)
        nc.gpsimd.memset(w5_sc[:].bitcast(I32), 0)
        load_weight_scales(nc.gpsimd, w5_sc, w5_scales)

        tab_w = [load_table(0)]
        w2_raw = sb("w2_raw", [P, PASSES, 2 * H], U8)
        nc.sync.dma_start(w2_raw[:].bitcast(I32), w2_words.rearrange("a p n -> p a n").bitcast(I32))
        w1_raw = [load_rows(placed("w1_raw0", [P, PACK, H], F32, 7168), w1, 0)]
        load_weight_scales(nc.sync, w2_sc_raw, w2_scales)
        tab_w.append(load_table(1))
        w1_raw.append(load_rows(placed("w1_raw1", [P, PACK, H], F32, 22528), w1, 1))

        v = {}
        sc12 = sb("sc12", [P, 2, S], U8)
        sc3 = sb("sc3", [P, S], U8)
        nc.vector.tensor_copy(sc12[:, 0, :], tab_sc[:].indirect(lists["acceptor"][:]))
        nc.vector.tensor_copy(sc12[:, 1, :], tab_sc[:].indirect(lists["donor"][:]))
        for q in range(QUADS):
            nc.sync.dma_start(
                moved_sc[32 * q : 32 * q + 4, :, :].bitcast(I32), sc12[32 * q + 4 : 32 * q + 8, :, :].bitcast(I32)
            )

        w1_bf = [sb("w1_bf%d" % a, [P, H * PACK], BF16) for a in range(PASSES)]
        round_first_stage(nc.scalar, w1_bf[0], w1_raw[0], 0, PACK)
        round_first_stage(nc.scalar, w1_bf[1], w1_raw[1], 0, PACK // 2)

        nc.vector.tensor_copy(sc3[:], tab_sc[:].indirect(lists["additive"][:]))
        w2_w = sb("w2_w", [P, PASSES, 2 * H], U8, "tab_sc")
        w2_sc = sb("w2_sc", [P, PASSES, H], U8)
        nc.vector.tensor_copy(
            w2_w[:].bitcast(I32).rearrange("p a (t u w) -> p a t u w", t=PACK, w=2),
            w2_raw[:].bitcast(I32).rearrange("p a (u t w) -> p a t u w", t=PACK, w=2),
        )
        w3_raw = [
            load_rows(placed("w3_raw0", [P, PACK, H], F32, 0), w3, 0),
            load_rows(placed("w3_raw1", [P, PACK, H], F32, 14336), w3, 1),
        ]
        base_t = placed("base_t", [P, N_TILES], F32, 11264)
        gain_t = [placed("gain_t%d" % t, [P, 1], F32, 22528 + 64 * t) for t in range(PACK)]
        with nc.allow_non_contiguous_dma(reason="one value a partition and tile"):
            nc.sync.dma_start(base_t[:], base.rearrange("(c p) -> p c", p=P))
        w4_rows = w4.rearrange("(u t e) n -> t u e n", t=PACK, e=RUN)
        w4_raw = placed("w4_raw", [P, W4_PARTS, PACK, W4_COLS], F32, 23552)
        for c in range(W4_PARTS):
            for t in range(PACK):
                nc.sync.dma_start(w4_raw[:, c, t, :], w4_rows[t][:, :, c * W4_COLS : (c + 1) * W4_COLS])
        with nc.allow_non_contiguous_dma(reason="one value a partition"):
            for t in range(PACK):
                nc.sync.dma_start(gain_t[t][:], gain.rearrange("(u t e) -> t u e", t=PACK, e=RUN)[t])
        nc.vector.tensor_copy(
            w2_sc[:].bitcast(I32).rearrange("p a (t u) -> p a t u", t=PACK),
            w2_sc_raw[:].bitcast(I32).rearrange("p a (u t) -> p a t u", t=PACK),
        )
        for a in range(PASSES):
            for name in ("acceptor", "donor", "additive"):
                gather_words(name, a)
        round_first_stage(nc.vector, w1_bf[1], w1_raw[1], PACK // 2, PACK)
        w1_q = [quantise("w1_%d" % a, w1_bf[a], H) for a in range(PASSES)]

        v_sc = {
            ("acceptor", 0): sc12[:, 0, :],
            ("acceptor", 1): moved_sc[:, 0, :],
            ("donor", 0): sc12[:, 1, :],
            ("donor", 1): moved_sc[:, 1, :],
            ("additive", 0): sc3[:],
            ("additive", 1): sc3[4:P, :],
        }

        def product(acc, name, a, lhs, lhs_sc, start, stop):
            nc.tensor.matmul_mx(
                out=acc, lhsT=lhs, lhsT_scale=lhs_sc, rhs=v[name, a][:].bitcast(FP8X4),
                rhs_scale=v_sc[name, a], start=start, stop=stop,
            )


        acceptor = [bank(t, "acceptor%d" % t) for t in range(PACK)]
        acc_sb = []
        for a in range(PASSES):
            for t in range(PACK):
                product(acceptor[t][:], "acceptor", a, w2_w[:, a, 2 * P * t : 2 * P * (t + 1)].bitcast(FP4X4),
                        w2_sc[:, a, P * t : P * (t + 1)], a == 0, a == PASSES - 1)
        for t in range(PACK):
            held = sb("acceptor_sb%d" % t, [P, S], F32)
            nc.scalar.copy(held[:], acceptor[t][:])
            acc_sb.append(held)

        w3_bf0 = sb("w3_bf0", [P, H * PACK], BF16)
        round_first_stage(nc.scalar, w3_bf0, w3_raw[0], 0, PACK)
        w5_w = placed("w5_w", [P, PASSES, 2 * N], U8, 3072)
        nc.sync.dma_start(w5_w[:].bitcast(I32), w5_words.rearrange("a p n -> p a n").bitcast(I32))
        w4_bf0 = placed("w4_bf0", [P, W4_COLS * PACK], BF16, 0)
        interleave(nc.scalar, w4_bf0[:], w4_raw[:, 0])

        donor = [bank(PACK + t, "donor%d" % t) for t in range(PACK)]
        for a in range(PASSES):
            codes, scales = w1_q[a]
            for t in range(PACK):
                product(donor[t][:], "donor", a, codes[:, P * t : P * (t + 1)].bitcast(FP8X4),
                        scales[:, P * t : P * (t + 1)], a == 0, a == PASSES - 1)
        larger = []
        for t in range(PACK):
            top = sb("larger%d" % t, [P, S], F32)
            nc.vector.tensor_tensor(top[:], donor[t][:], acc_sb[t][:], ALU.max)
            larger.append(top)

        w3_bf1 = sb("w3_bf1", [P, H * PACK], BF16)
        round_first_stage(nc.vector, w3_bf1, w3_raw[1], 0, PACK)
        w3_q = {1: quantise("w3_1", w3_bf1, H), 0: quantise("w3_0", w3_bf0, H)}

        scores = []

        def open_scores(m):
            acc = bank(m, "score%d" % m)
            for a in range(PASSES):
                product(acc[:], "donor", a, w5_w[:, a, 2 * P * m : 2 * P * (m + 1)].bitcast(FP4X4),
                        w5_sc[:, a, P * m : P * (m + 1)], a == 0, False)
            scores.append(acc)

        additive = [bank(PACK + t, "additive%d" % t) for t in range(PACK)]
        for first in range(0, PACK, 2):
            for a in (1, 0):
                codes, scales = w3_q[a]
                for t in (first, first + 1):
                    product(additive[t][:], "additive", a, codes[:, P * t : P * (t + 1)].bitcast(FP8X4),
                            scales[:, P * t : P * (t + 1)], a == 1, a == 0)

        w4_bf1 = sb("w4_bf1", [P, W4_COLS * PACK], BF16, "w3_bf0")
        interleave(nc.vector, w4_bf1[:], w4_raw[:, 1])
        w4_q = [quantise("w4_0", w4_bf0, W4_COLS)]

        h32 = sb("h32", [P, PACK, S], F32)
        for t in range(PACK):
            wave = sb("wave%d" % t, [P, S], F32)
            nc.scalar.activation(wave[:], additive[t][:], ACT.Sin)
            nc.vector.scalar_tensor_tensor(h32[:, t, :], wave[:], gain_t[t][:], larger[t][:], ALU.mult, ALU.add)
        for m in range(N_TILES):
            open_scores(m)
        h_bf = sb("h_bf", [P, S * PACK], BF16)
        interleave(nc.vector, h_bf[:, : H_SPLIT * PACK], h32[:, :, :H_SPLIT])
        interleave(nc.scalar, h_bf[:, H_SPLIT * PACK :], h32[:, :, H_SPLIT:])
        h_codes, h_scales = quantise("h", h_bf, S)
        w4_q.append(quantise("w4_1", w4_bf1, W4_COLS))

        for m in range(N_TILES):
            c, first = divmod(m * P, W4_COLS)
            codes, scales = w4_q[c]
            nc.tensor.matmul_mx(
                out=scores[m][:], lhsT=codes[:, first : first + P].bitcast(FP8X4),
                lhsT_scale=scales[:, first : first + P], rhs=h_codes[:].bitcast(FP8X4),
                rhs_scale=h_scales[:], start=False, stop=True,
            )
        for m in range(N_TILES):
            result = sb("result%d" % m, [P, S], F32)
            if m % 2 == 0:
                nc.scalar.activation(result[:], scores[m][:], ACT.Identity, bias=base_t[:, m : m + 1])
            else:
                nc.vector.tensor_scalar_add(result[:], scores[m][:], base_t[:, m : m + 1])
            nc.sync.dma_start(out[m * P : (m + 1) * P, :], result[:])
